import numpy as np
import ml_dtypes


def mxq(x, axis, fmt="e4m3"):
    dtype, down = {"e4m3": (ml_dtypes.float8_e4m3fn, 7), "e5m2": (ml_dtypes.float8_e5m2, 14)}[fmt]
    v = np.moveaxis(np.asarray(x, np.float32).astype(ml_dtypes.bfloat16).astype(np.float64), axis, -1)
    blocks = v.reshape(v.shape[:-1] + (-1, 32))
    amax = np.abs(blocks).max(-1, keepdims=True)
    byte = np.maximum(np.where(amax > 0, np.frexp(amax)[1] - 1 + 127, 0) - down, 1)
    scale = np.exp2(byte - 127.0)
    codes = (blocks / scale).astype(np.float32).astype(dtype).astype(np.float64)
    return np.moveaxis((codes * scale).reshape(v.shape), -1, axis)


WIDE = False


def mx_kscale(k):
    if not WIDE:
        return np.ones(k)
    levels = np.array([10, -10, 5, -5, 0])
    if k % 512:
        return np.exp2(np.random.permutation(np.resize(levels, k // 32))).repeat(32)
    a = np.empty((k // 512, 16))
    for p in range(k // 512):
        a[p, :8] = np.random.permutation(np.resize(levels, 8))
        for g in range(8):
            far = levels[np.abs(levels - a[p, g]) >= 10]
            a[p, g + 8] = far[np.random.randint(len(far))]
    return np.exp2(a.ravel()).repeat(32)


def f64(x):
    return np.asarray(x).astype(np.float64)


def striped(idx):
    return np.tile(np.asarray(idx).reshape(-1, 16).T, (8, 1)).astype(np.uint16)


def unstriped(offs):
    return offs[:16].T.reshape(-1).astype(np.int64)


E2M1 = np.array([0.0, 0.5, 1.0, 1.5, 2.0, 3.0, 4.0, 6.0, -0.0, -0.5, -1.0, -1.5, -2.0, -3.0, -4.0, -6.0])


def pack_weight(w, fmt):
    k, n = w.shape
    w = f64(np.asarray(w, np.float32).astype(ml_dtypes.bfloat16)).reshape(k // 32, 32, n)
    amax = np.abs(w).max(1)
    if fmt == "e4m3":
        byte = np.frexp(amax)[1] - 1 + 127 - 7
    else:
        mant, ex = np.frexp(amax / 6.0)
        byte = np.where(mant > 0.5, ex, ex - 1) + 127
    byte = np.clip(np.where(amax > 0, byte, 1), 1, 254)
    scaled = (w * np.exp2(127.0 - byte)[:, None, :]).reshape(k, n).astype(np.float32)
    by_word = np.ascontiguousarray(scaled.reshape(k // 512, 128, 4, n).transpose(0, 1, 3, 2))
    if fmt == "e4m3":
        words = by_word.astype(ml_dtypes.float8_e4m3fn).view(np.uint8)
    else:
        c = by_word.astype(ml_dtypes.float4_e2m1fn).view(np.uint8) & 0xF
        words = (c[..., 0::2] | (c[..., 1::2] << 4)).reshape(k // 512, 128, 2 * n)
    return np.ascontiguousarray(words), np.ascontiguousarray(byte.astype(np.uint8).reshape(k // 512, 16, n))


def unpack_weight(words, scales, fmt):
    g, _, n = scales.shape
    words = np.ascontiguousarray(words).reshape(g, 128, n, -1)
    if fmt == "e4m3":
        vals = words.view(ml_dtypes.float8_e4m3fn).astype(np.float64)
    else:
        nib = np.empty((g, 128, n, 4), np.uint8)
        nib[..., 0::2] = words & 0xF
        nib[..., 1::2] = words >> 4
        vals = E2M1[nib]
    vals = vals * np.repeat(np.exp2(scales.astype(np.float64) - 127.0), 8, axis=1)[..., None]
    return vals.transpose(0, 1, 3, 2).reshape(g * 512, n)


K, L, T, J, N = 512, 512, 1024, 512, 512


def setup_inputs():
    n = np.random.standard_normal
    idx = np.random.permutation(T)[:J]
    fk = mx_kscale(K)
    fl = mx_kscale(L)
    xap = pack_weight(n((K, J)) / fk[:, None], "e2m1")
    wap = pack_weight(n((K, N)) * 1 / np.sqrt(K) * fk[:, None], "e4m3")
    wbp = pack_weight(n((L, N)) * 1 / np.sqrt(L) * fl[:, None], "e2m1")
    return {
        "xa_words": xap[0],
        "xa_scales": xap[1],
        "wa_words": wap[0],
        "wa_scales": wap[1],
        "xb": (n((L, J)) / fl[:, None]).astype(np.float32),
        "wb_words": wbp[0],
        "wb_scales": wbp[1],
        "old": (1.0 * n((N, T))).astype(np.float32),
        "offs": striped(idx),
    }


def reference(xa_words, xa_scales, wa_words, wa_scales, xb, wb_words, wb_scales, old, offs):
    idx = unstriped(offs)
    xau = unpack_weight(xa_words, xa_scales, "e2m1")
    wau = unpack_weight(wa_words, wa_scales, "e4m3")
    wbu = unpack_weight(wb_words, wb_scales, "e2m1")
    xbq = mxq(f64(xb), 0, "e4m3")
    v = wau.T @ xau + wbu.T @ xbq
    fd = 0.9 * f64(old)
    d = np.maximum(v - fd[:, idx], 0.0)
    p = np.zeros((N, T))
    p[:, idx] = d
    y = fd + p
    return y

@@ -1,0 +1,149 @@
+from contextlib import ExitStack
+
+import concourse.mybir as mybir
+
+K, L, T, J, N = 512, 512, 1024, 512, 512
+FLOPS = 2 * N * J * (K + L)
+
+F32 = mybir.dt.float32
+BF16 = mybir.dt.bfloat16
+I32 = mybir.dt.int32
+U32 = mybir.dt.uint32
+U16 = mybir.dt.uint16
+U8 = mybir.dt.uint8
+FP8X4 = mybir.dt.float8_e4m3fn_x4
+FP4X4 = mybir.dt.float4_e2m1fn_x4
+ALU = mybir.AluOpType
+ACT = mybir.ActivationFunctionType
+
+P = 128
+PACK = 4
+TILES = N // P
+HALF = J // 2
+FADE = 0.9
+
+
+def tile_list_page_running_peak_kernel(tc, xa_words, xa_scales, wa_words, wa_scales, xb, wb_words, wb_scales, old, offs, out):
+    nc = tc.nc
+    with ExitStack() as ctx:
+        keep = ctx.enter_context(tc.tile_pool(name="keep", bufs=1))
+        psum = ctx.enter_context(tc.psum_pool(name="psum", bufs=1))
+
+        offsets = keep.tile([P, J // 16], U16, name="offsets")
+        planes = keep.tile([P, 3 * J], U8, name="planes", align_bytes=64)
+
+        pages = [keep.tile([P, T], F32, name=f"page{i}") for i in range(TILES)]
+        for page in pages:
+            nc.vector.memset(page[:], 0.0)
+
+        olds = [keep.tile([P, T], F32, name=f"old{i}") for i in range(TILES)]
+        raws = [keep.tile([P, PACK, HALF], F32, name=f"raw{h}") for h in range(2)]
+        xa_sb = keep.tile([P, 2 * J], U8, name="xa_sb", align_bytes=64)
+        wa_sb = keep.tile([P, 4 * N], U8, name="wa_sb", align_bytes=64)
+        wb_sb = keep.tile([P, 2 * N], U8, name="wb_sb", align_bytes=64)
+
+        for s, scales in enumerate((wb_scales, wa_scales, xa_scales)):
+            for q in range(4):
+                nc.scalar.dma_start(
+                    out=planes[32 * q : 32 * q + 4, s * J : (s + 1) * J].bitcast(I32),
+                    in_=scales[0, 4 * q : 4 * q + 4, :].bitcast(I32),
+                )
+        wb_plane = planes[:, 0:J]
+        wa_plane = planes[:, J : 2 * J]
+        xa_plane = planes[:, 2 * J : 3 * J]
+
+        xb_rows = xb.rearrange("(p r) j -> p r j", r=PACK)
+        nc.sync.dma_start(offsets[:], offs)
+        nc.sync.dma_start(out=olds[0][:], in_=old[0:P, :])
+        for h in range(2):
+            nc.sync.dma_start(out=raws[h][:], in_=xb_rows[:, :, h * HALF : (h + 1) * HALF])
+        nc.sync.dma_start(out=wa_sb[:].bitcast(I32), in_=wa_words[0].rearrange("p n t -> p (n t)").bitcast(I32))
+        nc.sync.dma_start(out=xa_sb[:].bitcast(I32), in_=xa_words[0].bitcast(I32))
+        nc.sync.dma_start(out=wb_sb[:].bitcast(I32), in_=wb_words[0].bitcast(I32))
+        for i in range(1, TILES):
+            nc.sync.dma_start(out=olds[i][:], in_=old[i * P : (i + 1) * P, :])
+
+        fds = [keep.tile([P, T], F32, name=f"fd{i}") for i in range(TILES)]
+        nc.vector.tensor_scalar(out=fds[0][:], in0=olds[0][:], scalar1=FADE, scalar2=None, op0=ALU.mult)
+        picked = keep.tile([P, J], F32, name="picked")
+        nc.vector.tensor_copy(picked[:], fds[0][:].indirect(offsets[:]))
+
+        xb_codes = keep.tile([P, J], U32, name="xb_codes", align_bytes=64)
+        xb_plane = keep.tile([P, J], U8, name="xb_plane", align_bytes=64)
+        grouped = [keep.tile([P, HALF, PACK], BF16, name=f"grouped{h}", align_bytes=64) for h in range(2)]
+        minus_picked = keep.tile([P, J], F32, name="minus_picked")
+        nc.scalar.mul(out=minus_picked[:], in_=picked[:], mul=-1.0)
+        for h in range(2):
+            cols = slice(h * HALF, (h + 1) * HALF)
+            nc.vector.tensor_copy(
+                out=grouped[h][:].rearrange("p (c i) r -> p c r i", i=4),
+                in_=raws[h][:].rearrange("p r (c i) -> p c r i", i=4),
+            )
+            nc.vector.quantize_mx(
+                out=xb_codes[:, cols].bitcast(FP8X4),
+                scales=xb_plane[:, cols],
+                in_=grouped[h][:].rearrange("p j r -> p (j r)"),
+            )
+
+        banks = [psum.tile([P, J], F32, name=f"bank{i}") for i in range(TILES)]
+
+        def pass_a(i, start, stop):
+            nc.tensor.matmul_mx(
+                out=banks[i][:],
+                lhsT=wa_sb[:, 4 * i * P : 4 * (i + 1) * P].bitcast(FP8X4),
+                lhsT_scale=wa_plane[:, i * P : (i + 1) * P],
+                rhs=xa_sb[:].bitcast(FP4X4),
+                rhs_scale=xa_plane,
+                start=start,
+                stop=stop,
+            )
+
+        def pass_b(i, cols, start, stop):
+            nc.tensor.matmul_mx(
+                out=banks[i][:, cols],
+                lhsT=wb_sb[:, 2 * i * P : 2 * (i + 1) * P].bitcast(FP4X4),
+                lhsT_scale=wb_plane[:, i * P : (i + 1) * P],
+                rhs=xb_codes[:, cols].bitcast(FP8X4),
+                rhs_scale=xb_plane[:, cols],
+                start=start,
+                stop=stop,
+            )
+
+        pass_a(0, True, False)
+        for c in range(J // P):
+            pass_b(0, slice(c * P, (c + 1) * P), False, c == J // P - 1)
+        for i in range(1, TILES):
+            pass_b(i, slice(0, J), True, False)
+            pass_a(i, False, True)
+
+        peak = keep.tile([P, J], F32, name="peak")
+        nc.vector.tensor_tensor(out=peak[:], in0=banks[0][:], in1=picked[:], op=ALU.max)
+        nc.vector.tensor_tensor(pages[0][:].indirect(offsets[:]), peak[:], minus_picked[:], ALU.add)
+
+        sums = {}
+        for i in range(1, TILES):
+            tag = "late" if i == TILES - 1 else f"sum{i}"
+            sums[i] = keep.tile([P, J], F32, name=f"sum{i}", tag=tag)
+            nc.scalar.copy(out=sums[i][:], in_=banks[i][:])
+        for i in range(1, TILES):
+            nc.scalar.mul(out=fds[i][:], in_=olds[i][:], mul=FADE)
+        gaps = {}
+        for i in range(1, TILES):
+            gaps[i] = keep.tile([P, J], F32, name=f"gap{i}")
+            nc.vector.tensor_tensor(gaps[i][:], fds[i][:].indirect(offsets[:]), sums[i][:], ALU.subtract)
+        for i in range(1, TILES):
+            rise = keep.tile([P, J], F32, name=f"rise{i}")
+            nc.scalar.activation(out=rise[:], in_=gaps[i][:], func=ACT.Relu, scale=-1.0)
+            nc.vector.tensor_copy(pages[i][:].indirect(offsets[:]), rise[:])
+
+        for i in range(TILES - 1):
+            tag = "late" if i == 0 else f"new{i}"
+            new = keep.tile([P, T], F32, name=f"new{i}", tag=tag)
+            nc.gpsimd.tensor_tensor(out=new[:], in0=fds[i][:], in1=pages[i][:], op=ALU.add)
+            nc.sync.dma_start(out=out[i * P : (i + 1) * P, :], in_=new[:])
+        i = TILES - 1
+        for h in range(2):
+            cols = slice(h * T // 2, (h + 1) * T // 2)
+            last = keep.tile([P, T // 2], F32, name=f"last{h}")
+            nc.vector.tensor_tensor(out=last[:], in0=fds[i][:, cols], in1=pages[i][:, cols], op=ALU.add)
+            nc.sync.dma_start(out=out[i * P : (i + 1) * P, cols], in_=last[:])

@@ -21,6 +21,8 @@ PACK = 4
 TILES = N // P
 HALF = J // 2
 FADE = 0.9
+WEAVE_SPLIT = 176
+FADE_SPLIT = 736
 
 
 def tile_list_page_running_peak_kernel(tc, xa_words, xa_scales, wa_words, wa_scales, xb, wb_words, wb_scales, old, offs, out):
@@ -32,58 +34,69 @@ def tile_list_page_running_peak_kernel(tc, xa_words, xa_scales, wa_words, wa_sca
         offsets = keep.tile([P, J // 16], U16, name="offsets")
         planes = keep.tile([P, 3 * J], U8, name="planes", align_bytes=64)
 
-        pages = [keep.tile([P, T], F32, name=f"page{i}") for i in range(TILES)]
-        for page in pages:
-            nc.vector.memset(page[:], 0.0)
+        pages = [keep.tile([P, T], F32, name="page0")]
+        nc.vector.memset(pages[0][:], 0.0)
 
-        olds = [keep.tile([P, T], F32, name=f"old{i}") for i in range(TILES)]
+        olds = [keep.tile([P, T], F32, name=f"old{i}", tag=f"old{i}") for i in range(TILES)]
         raws = [keep.tile([P, PACK, HALF], F32, name=f"raw{h}") for h in range(2)]
         xa_sb = keep.tile([P, 2 * J], U8, name="xa_sb", align_bytes=64)
         wa_sb = keep.tile([P, 4 * N], U8, name="wa_sb", align_bytes=64)
         wb_sb = keep.tile([P, 2 * N], U8, name="wb_sb", align_bytes=64)
-
-        for s, scales in enumerate((wb_scales, wa_scales, xa_scales)):
-            for q in range(4):
-                nc.scalar.dma_start(
-                    out=planes[32 * q : 32 * q + 4, s * J : (s + 1) * J].bitcast(I32),
-                    in_=scales[0, 4 * q : 4 * q + 4, :].bitcast(I32),
-                )
         wb_plane = planes[:, 0:J]
         wa_plane = planes[:, J : 2 * J]
         xa_plane = planes[:, 2 * J : 3 * J]
 
-        xb_rows = xb.rearrange("(p r) j -> p r j", r=PACK)
-        nc.sync.dma_start(offsets[:], offs)
-        nc.sync.dma_start(out=olds[0][:], in_=old[0:P, :])
-        for h in range(2):
-            nc.sync.dma_start(out=raws[h][:], in_=xb_rows[:, :, h * HALF : (h + 1) * HALF])
-        nc.sync.dma_start(out=wa_sb[:].bitcast(I32), in_=wa_words[0].rearrange("p n t -> p (n t)").bitcast(I32))
-        nc.sync.dma_start(out=xa_sb[:].bitcast(I32), in_=xa_words[0].bitcast(I32))
-        nc.sync.dma_start(out=wb_sb[:].bitcast(I32), in_=wb_words[0].bitcast(I32))
-        for i in range(1, TILES):
+        def load_scale_rows(queue, plane, scales, q):
+            queue.dma_start(
+                out=plane[32 * q : 32 * q + 4, :].bitcast(I32),
+                in_=scales[0, 4 * q : 4 * q + 4, :].bitcast(I32),
+            )
+
+        def load_old(i):
             nc.sync.dma_start(out=olds[i][:], in_=old[i * P : (i + 1) * P, :])
 
-        fds = [keep.tile([P, T], F32, name=f"fd{i}") for i in range(TILES)]
-        nc.vector.tensor_scalar(out=fds[0][:], in0=olds[0][:], scalar1=FADE, scalar2=None, op0=ALU.mult)
-        picked = keep.tile([P, J], F32, name="picked")
-        nc.vector.tensor_copy(picked[:], fds[0][:].indirect(offsets[:]))
+        xb_rows = xb.rearrange("(p r) j -> p r j", r=PACK)
+        for q in range(4):
+            load_scale_rows(nc.gpsimd, xa_plane, xa_scales, q)
+        nc.sync.dma_start(out=raws[0][:], in_=xb_rows[:, :, 0:HALF])
+        nc.sync.dma_start(offsets[:], offs)
+        for q in range(4):
+            load_scale_rows(nc.sync, wb_plane, wb_scales, q)
+        nc.sync.dma_start(out=raws[1][:], in_=xb_rows[:, :, HALF:J])
+        load_old(0)
+        nc.sync.dma_start(out=wb_sb[:].bitcast(I32), in_=wb_words[0].bitcast(I32))
+        for q in range(4):
+            load_scale_rows(nc.sync, wa_plane, wa_scales, q)
+        nc.sync.dma_start(out=xa_sb[:].bitcast(I32), in_=xa_words[0].bitcast(I32))
+        nc.sync.dma_start(out=wa_sb[:].bitcast(I32), in_=wa_words[0].rearrange("p n t -> p (n t)").bitcast(I32))
+        for i in range(1, TILES):
+            load_old(i)
 
         xb_codes = keep.tile([P, J], U32, name="xb_codes", align_bytes=64)
         xb_plane = keep.tile([P, J], U8, name="xb_plane", align_bytes=64)
-        grouped = [keep.tile([P, HALF, PACK], BF16, name=f"grouped{h}", align_bytes=64) for h in range(2)]
-        minus_picked = keep.tile([P, J], F32, name="minus_picked")
-        nc.scalar.mul(out=minus_picked[:], in_=picked[:], mul=-1.0)
         for h in range(2):
+            grouped = keep.tile([P, HALF, PACK], BF16, name=f"grouped{h}", align_bytes=64)
+            for copy, a, b in ((nc.scalar.copy, WEAVE_SPLIT, HALF), (nc.vector.tensor_copy, 0, WEAVE_SPLIT)):
+                copy(
+                    out=grouped[:, a:b, :].rearrange("p (c i) r -> p c r i", i=4),
+                    in_=raws[h][:, :, a:b].rearrange("p r (c i) -> p c r i", i=4),
+                )
             cols = slice(h * HALF, (h + 1) * HALF)
-            nc.vector.tensor_copy(
-                out=grouped[h][:].rearrange("p (c i) r -> p c r i", i=4),
-                in_=raws[h][:].rearrange("p r (c i) -> p c r i", i=4),
-            )
             nc.vector.quantize_mx(
                 out=xb_codes[:, cols].bitcast(FP8X4),
                 scales=xb_plane[:, cols],
-                in_=grouped[h][:].rearrange("p j r -> p (j r)"),
+                in_=grouped[:].rearrange("p j r -> p (j r)"),
             )
+
+        fds = [keep.tile([P, T], F32, name=f"fd{i}") for i in range(TILES)]
+        nc.vector.tensor_scalar(out=fds[0][:, 0:FADE_SPLIT], in0=olds[0][:, 0:FADE_SPLIT], scalar1=FADE, scalar2=None, op0=ALU.mult)
+        nc.scalar.mul(out=fds[0][:, FADE_SPLIT:T], in_=olds[0][:, FADE_SPLIT:T], mul=FADE)
+        picked = keep.tile([P, J], F32, name="picked", tag="picked")
+        minus_picked = keep.tile([P, J], F32, name="minus_picked", tag="minus_picked")
+        for h in range(2):
+            cols = slice(h * HALF, (h + 1) * HALF)
+            nc.vector.tensor_copy(picked[:, cols], fds[0][:].indirect(offsets[:, h * HALF // 16 : (h + 1) * HALF // 16]))
+            nc.scalar.mul(out=minus_picked[:, cols], in_=picked[:, cols], mul=-1.0)
 
         banks = [psum.tile([P, J], F32, name=f"bank{i}") for i in range(TILES)]
 
@@ -98,52 +111,60 @@ def tile_list_page_running_peak_kernel(tc, xa_words, xa_scales, wa_words, wa_sca
                 stop=stop,
             )
 
-        def pass_b(i, cols, start, stop):
+        def pass_b(i, start, stop):
             nc.tensor.matmul_mx(
-                out=banks[i][:, cols],
+                out=banks[i][:],
                 lhsT=wb_sb[:, 2 * i * P : 2 * (i + 1) * P].bitcast(FP4X4),
                 lhsT_scale=wb_plane[:, i * P : (i + 1) * P],
-                rhs=xb_codes[:, cols].bitcast(FP8X4),
-                rhs_scale=xb_plane[:, cols],
+                rhs=xb_codes[:].bitcast(FP8X4),
+                rhs_scale=xb_plane[:],
                 start=start,
                 stop=stop,
             )
 
-        pass_a(0, True, False)
-        for c in range(J // P):
-            pass_b(0, slice(c * P, (c + 1) * P), False, c == J // P - 1)
+        pass_b(0, True, False)
+        pass_a(0, False, True)
         for i in range(1, TILES):
-            pass_b(i, slice(0, J), True, False)
-            pass_a(i, False, True)
+            pass_a(i, True, False)
+            pass_b(i, False, True)
 
-        peak = keep.tile([P, J], F32, name="peak")
+        peak = keep.tile([P, J], F32, name="peak", tag="peak")
         nc.vector.tensor_tensor(out=peak[:], in0=banks[0][:], in1=picked[:], op=ALU.max)
         nc.vector.tensor_tensor(pages[0][:].indirect(offsets[:]), peak[:], minus_picked[:], ALU.add)
+
+        for i, tag in enumerate(("picked", "minus_picked", "peak")):
+            page = keep.tile([P, T], F32, name=f"page{i + 1}", tag=tag)
+            nc.gpsimd.memset(page[:], 0.0)
+            pages.append(page)
 
         sums = {}
         for i in range(1, TILES):
             tag = "late" if i == TILES - 1 else f"sum{i}"
             sums[i] = keep.tile([P, J], F32, name=f"sum{i}", tag=tag)
-            nc.scalar.copy(out=sums[i][:], in_=banks[i][:])
-        for i in range(1, TILES):
             nc.scalar.mul(out=fds[i][:], in_=olds[i][:], mul=FADE)
+            nc.scalar.copy(out=sums[i][:], in_=banks[i][:])
         gaps = {}
         for i in range(1, TILES):
             gaps[i] = keep.tile([P, J], F32, name=f"gap{i}")
             nc.vector.tensor_tensor(gaps[i][:], fds[i][:].indirect(offsets[:]), sums[i][:], ALU.subtract)
-        for i in range(1, TILES):
-            rise = keep.tile([P, J], F32, name=f"rise{i}")
-            nc.scalar.activation(out=rise[:], in_=gaps[i][:], func=ACT.Relu, scale=-1.0)
-            nc.vector.tensor_copy(pages[i][:].indirect(offsets[:]), rise[:])
 
-        for i in range(TILES - 1):
+        def finish(i):
             tag = "late" if i == 0 else f"new{i}"
             new = keep.tile([P, T], F32, name=f"new{i}", tag=tag)
             nc.gpsimd.tensor_tensor(out=new[:], in0=fds[i][:], in1=pages[i][:], op=ALU.add)
             nc.sync.dma_start(out=out[i * P : (i + 1) * P, :], in_=new[:])
+
+        for i in range(1, TILES):
+            tag = "old3" if i == 1 else f"rise{i}"
+            rise = keep.tile([P, J], F32, name=f"rise{i}", tag=tag)
+            nc.scalar.activation(out=rise[:], in_=gaps[i][:], func=ACT.Relu, scale=-1.0)
+            finish(i - 1)
+            nc.vector.tensor_copy(pages[i][:].indirect(offsets[:]), rise[:])
+
         i = TILES - 1
-        for h in range(2):
-            cols = slice(h * T // 2, (h + 1) * T // 2)
-            last = keep.tile([P, T // 2], F32, name=f"last{h}")
+        width = T // 4
+        for h in range(4):
+            cols = slice(h * width, (h + 1) * width)
+            last = keep.tile([P, width], F32, name=f"last{h}")
             nc.vector.tensor_tensor(out=last[:], in0=fds[i][:, cols], in1=pages[i][:, cols], op=ALU.add)
-            nc.sync.dma_start(out=out[i * P : (i + 1) * P, cols], in_=last[:])
+            nc.scalar.dma_start(out=out[i * P : (i + 1) * P, cols], in_=last[:])

@@ -32,19 +32,16 @@ def tile_list_page_running_peak_kernel(tc, xa_words, xa_scales, wa_words, wa_sca
         psum = ctx.enter_context(tc.psum_pool(name="psum", bufs=1))
 
         offsets = keep.tile([P, J // 16], U16, name="offsets")
-        planes = keep.tile([P, 3 * J], U8, name="planes", align_bytes=64)
 
-        pages = [keep.tile([P, T], F32, name="page0")]
-        nc.vector.memset(pages[0][:], 0.0)
 
         olds = [keep.tile([P, T], F32, name=f"old{i}", tag=f"old{i}") for i in range(TILES)]
         raws = [keep.tile([P, PACK, HALF], F32, name=f"raw{h}") for h in range(2)]
         xa_sb = keep.tile([P, 2 * J], U8, name="xa_sb", align_bytes=64)
         wa_sb = keep.tile([P, 4 * N], U8, name="wa_sb", align_bytes=64)
         wb_sb = keep.tile([P, 2 * N], U8, name="wb_sb", align_bytes=64)
-        wb_plane = planes[:, 0:J]
-        wa_plane = planes[:, J : 2 * J]
-        xa_plane = planes[:, 2 * J : 3 * J]
+        xa_plane = keep.tile([P, J], U8, name="xa_plane", align_bytes=64)
+        wa_plane = keep.tile([P, N], U8, name="wa_plane", align_bytes=64)
+        wb_plane = keep.tile([P, N], U8, name="wb_plane", align_bytes=64)
 
         def load_scale_rows(queue, plane, scales, q):
             queue.dma_start(
@@ -91,6 +88,8 @@ def tile_list_page_running_peak_kernel(tc, xa_words, xa_scales, wa_words, wa_sca
         fds = [keep.tile([P, T], F32, name=f"fd{i}") for i in range(TILES)]
         nc.vector.tensor_scalar(out=fds[0][:, 0:FADE_SPLIT], in0=olds[0][:, 0:FADE_SPLIT], scalar1=FADE, scalar2=None, op0=ALU.mult)
         nc.scalar.mul(out=fds[0][:, FADE_SPLIT:T], in_=olds[0][:, FADE_SPLIT:T], mul=FADE)
+        pages = [keep.tile([P, T], F32, name="page0", tag="old0")]
+        nc.gpsimd.memset(pages[0][:], 0.0)
         picked = keep.tile([P, J], F32, name="picked", tag="picked")
         minus_picked = keep.tile([P, J], F32, name="minus_picked", tag="minus_picked")
         for h in range(2):
@@ -106,7 +105,7 @@ def tile_list_page_running_peak_kernel(tc, xa_words, xa_scales, wa_words, wa_sca
                 lhsT=wa_sb[:, 4 * i * P : 4 * (i + 1) * P].bitcast(FP8X4),
                 lhsT_scale=wa_plane[:, i * P : (i + 1) * P],
                 rhs=xa_sb[:].bitcast(FP4X4),
-                rhs_scale=xa_plane,
+                rhs_scale=xa_plane[:],
                 start=start,
                 stop=stop,
             )

@@ -18,11 +18,15 @@ ACT = mybir.ActivationFunctionType
 
 P = 128
 PACK = 4
+QUADRANTS = 4
+GROUP = 16
 TILES = N // P
+LAST = TILES - 1
 HALF = J // 2
 FADE = 0.9
 WEAVE_SPLIT = 176
 FADE_SPLIT = 736
+TAIL_PIECES = 4
 
 
 def tile_list_page_running_peak_kernel(tc, xa_words, xa_scales, wa_words, wa_scales, xb, wb_words, wb_scales, old, offs, out):
@@ -31,9 +35,7 @@ def tile_list_page_running_peak_kernel(tc, xa_words, xa_scales, wa_words, wa_sca
         keep = ctx.enter_context(tc.tile_pool(name="keep", bufs=1))
         psum = ctx.enter_context(tc.psum_pool(name="psum", bufs=1))
 
-        offsets = keep.tile([P, J // 16], U16, name="offsets")
-
-
+        offsets = keep.tile([P, J // GROUP], U16, name="offsets")
         olds = [keep.tile([P, T], F32, name=f"old{i}", tag=f"old{i}") for i in range(TILES)]
         raws = [keep.tile([P, PACK, HALF], F32, name=f"raw{h}") for h in range(2)]
         xa_sb = keep.tile([P, 2 * J], U8, name="xa_sb", align_bytes=64)
@@ -43,27 +45,25 @@ def tile_list_page_running_peak_kernel(tc, xa_words, xa_scales, wa_words, wa_sca
         wa_plane = keep.tile([P, N], U8, name="wa_plane", align_bytes=64)
         wb_plane = keep.tile([P, N], U8, name="wb_plane", align_bytes=64)
 
-        def load_scale_rows(queue, plane, scales, q):
-            queue.dma_start(
-                out=plane[32 * q : 32 * q + 4, :].bitcast(I32),
-                in_=scales[0, 4 * q : 4 * q + 4, :].bitcast(I32),
-            )
+        def load_plane(queue, plane, scales):
+            for q in range(QUADRANTS):
+                queue.dma_start(
+                    out=plane[32 * q : 32 * q + 4, :].bitcast(I32),
+                    in_=scales[0, 4 * q : 4 * q + 4, :].bitcast(I32),
+                )
 
         def load_old(i):
             nc.sync.dma_start(out=olds[i][:], in_=old[i * P : (i + 1) * P, :])
 
         xb_rows = xb.rearrange("(p r) j -> p r j", r=PACK)
-        for q in range(4):
-            load_scale_rows(nc.gpsimd, xa_plane, xa_scales, q)
+        load_plane(nc.gpsimd, xa_plane, xa_scales)
         nc.sync.dma_start(out=raws[0][:], in_=xb_rows[:, :, 0:HALF])
         nc.sync.dma_start(offsets[:], offs)
-        for q in range(4):
-            load_scale_rows(nc.sync, wb_plane, wb_scales, q)
+        load_plane(nc.sync, wb_plane, wb_scales)
         nc.sync.dma_start(out=raws[1][:], in_=xb_rows[:, :, HALF:J])
         load_old(0)
         nc.sync.dma_start(out=wb_sb[:].bitcast(I32), in_=wb_words[0].bitcast(I32))
-        for q in range(4):
-            load_scale_rows(nc.sync, wa_plane, wa_scales, q)
+        load_plane(nc.sync, wa_plane, wa_scales)
         nc.sync.dma_start(out=xa_sb[:].bitcast(I32), in_=xa_words[0].bitcast(I32))
         nc.sync.dma_start(out=wa_sb[:].bitcast(I32), in_=wa_words[0].rearrange("p n t -> p (n t)").bitcast(I32))
         for i in range(1, TILES):
@@ -73,10 +73,10 @@ def tile_list_page_running_peak_kernel(tc, xa_words, xa_scales, wa_words, wa_sca
         xb_plane = keep.tile([P, J], U8, name="xb_plane", align_bytes=64)
         for h in range(2):
             grouped = keep.tile([P, HALF, PACK], BF16, name=f"grouped{h}", align_bytes=64)
-            for copy, a, b in ((nc.scalar.copy, WEAVE_SPLIT, HALF), (nc.vector.tensor_copy, 0, WEAVE_SPLIT)):
+            for copy, first, end in ((nc.scalar.copy, WEAVE_SPLIT, HALF), (nc.vector.tensor_copy, 0, WEAVE_SPLIT)):
                 copy(
-                    out=grouped[:, a:b, :].rearrange("p (c i) r -> p c r i", i=4),
-                    in_=raws[h][:, :, a:b].rearrange("p r (c i) -> p c r i", i=4),
+                    out=grouped[:, first:end, :].rearrange("p (c i) r -> p c r i", i=4),
+                    in_=raws[h][:, :, first:end].rearrange("p r (c i) -> p c r i", i=4),
                 )
             cols = slice(h * HALF, (h + 1) * HALF)
             nc.vector.quantize_mx(
@@ -94,7 +94,7 @@ def tile_list_page_running_peak_kernel(tc, xa_words, xa_scales, wa_words, wa_sca
         minus_picked = keep.tile([P, J], F32, name="minus_picked", tag="minus_picked")
         for h in range(2):
             cols = slice(h * HALF, (h + 1) * HALF)
-            nc.vector.tensor_copy(picked[:, cols], fds[0][:].indirect(offsets[:, h * HALF // 16 : (h + 1) * HALF // 16]))
+            nc.vector.tensor_copy(picked[:, cols], fds[0][:].indirect(offsets[:, h * HALF // GROUP : (h + 1) * HALF // GROUP]))
             nc.scalar.mul(out=minus_picked[:, cols], in_=picked[:, cols], mul=-1.0)
 
         banks = [psum.tile([P, J], F32, name=f"bank{i}") for i in range(TILES)]
@@ -136,34 +136,37 @@ def tile_list_page_running_peak_kernel(tc, xa_words, xa_scales, wa_words, wa_sca
             nc.gpsimd.memset(page[:], 0.0)
             pages.append(page)
 
-        sums = {}
-        for i in range(1, TILES):
-            tag = "late" if i == TILES - 1 else f"sum{i}"
-            sums[i] = keep.tile([P, J], F32, name=f"sum{i}", tag=tag)
-            nc.scalar.mul(out=fds[i][:], in_=olds[i][:], mul=FADE)
-            nc.scalar.copy(out=sums[i][:], in_=banks[i][:])
+        nc.scalar.mul(out=fds[1][:], in_=olds[1][:], mul=FADE)
+        sum_one = keep.tile([P, J], F32, name="sum_one", tag="old1")
+        nc.scalar.copy(out=sum_one[:], in_=banks[1][:])
+        nc.scalar.mul(out=fds[2][:], in_=olds[2][:], mul=FADE)
+        sum_pair = keep.tile([P, 2 * J], F32, name="sum_pair", tag="old2")
+        sums = {1: sum_one[:], 2: sum_pair[:, 0:J], 3: sum_pair[:, J : 2 * J]}
+        nc.scalar.copy(out=sums[2], in_=banks[2][:])
+        nc.scalar.copy(out=sums[3], in_=banks[3][:])
+        nc.scalar.mul(out=fds[3][:], in_=olds[3][:], mul=FADE)
+
         gaps = {}
         for i in range(1, TILES):
             gaps[i] = keep.tile([P, J], F32, name=f"gap{i}")
-            nc.vector.tensor_tensor(gaps[i][:], fds[i][:].indirect(offsets[:]), sums[i][:], ALU.subtract)
+            nc.vector.tensor_tensor(gaps[i][:], fds[i][:].indirect(offsets[:]), sums[i], ALU.subtract)
 
-        def finish(i):
-            tag = "late" if i == 0 else f"new{i}"
+        def add_and_store(i):
+            tag = "old2" if i == 0 else f"new{i}"
             new = keep.tile([P, T], F32, name=f"new{i}", tag=tag)
             nc.gpsimd.tensor_tensor(out=new[:], in0=fds[i][:], in1=pages[i][:], op=ALU.add)
             nc.sync.dma_start(out=out[i * P : (i + 1) * P, :], in_=new[:])
 
+        rises = keep.tile([P, LAST * J], F32, name="rises", tag="old3")
         for i in range(1, TILES):
-            tag = "old3" if i == 1 else f"rise{i}"
-            rise = keep.tile([P, J], F32, name=f"rise{i}", tag=tag)
-            nc.scalar.activation(out=rise[:], in_=gaps[i][:], func=ACT.Relu, scale=-1.0)
-            finish(i - 1)
-            nc.vector.tensor_copy(pages[i][:].indirect(offsets[:]), rise[:])
+            rise = rises[:, (i - 1) * J : i * J]
+            nc.scalar.activation(out=rise, in_=gaps[i][:], func=ACT.Relu, scale=-1.0)
+            add_and_store(i - 1)
+            nc.vector.tensor_copy(pages[i][:].indirect(offsets[:]), rise)
 
-        i = TILES - 1
-        width = T // 4
-        for h in range(4):
-            cols = slice(h * width, (h + 1) * width)
-            last = keep.tile([P, width], F32, name=f"last{h}")
-            nc.vector.tensor_tensor(out=last[:], in0=fds[i][:, cols], in1=pages[i][:, cols], op=ALU.add)
-            nc.scalar.dma_start(out=out[i * P : (i + 1) * P, cols], in_=last[:])
+        width = T // TAIL_PIECES
+        for piece in range(TAIL_PIECES):
+            cols = slice(piece * width, (piece + 1) * width)
+            tail = keep.tile([P, width], F32, name=f"tail{piece}")
+            nc.vector.tensor_tensor(out=tail[:], in0=fds[LAST][:, cols], in1=pages[LAST][:, cols], op=ALU.add)
+            nc.scalar.dma_start(out=out[LAST * P : N, cols], in_=tail[:])

from contextlib import ExitStack

import concourse.mybir as mybir

K, L, T, J, N = 512, 512, 1024, 512, 512
FLOPS = 2 * N * J * (K + L)

F32 = mybir.dt.float32
BF16 = mybir.dt.bfloat16
I32 = mybir.dt.int32
U32 = mybir.dt.uint32
U16 = mybir.dt.uint16
U8 = mybir.dt.uint8
FP8X4 = mybir.dt.float8_e4m3fn_x4
FP4X4 = mybir.dt.float4_e2m1fn_x4
ALU = mybir.AluOpType
ACT = mybir.ActivationFunctionType

P = 128
PACK = 4
QUADRANTS = 4
GROUP = 16
TILES = N // P
LAST = TILES - 1
HALF = J // 2
FADE = 0.9
WEAVE_SPLIT = 176
FADE_SPLIT = 736
TAIL_PIECES = 4


def tile_list_page_running_peak_kernel(tc, xa_words, xa_scales, wa_words, wa_scales, xb, wb_words, wb_scales, old, offs, out):
    nc = tc.nc
    with ExitStack() as ctx:
        keep = ctx.enter_context(tc.tile_pool(name="keep", bufs=1))
        psum = ctx.enter_context(tc.psum_pool(name="psum", bufs=1))

        offsets = keep.tile([P, J // GROUP], U16, name="offsets")
        olds = [keep.tile([P, T], F32, name=f"old{i}", tag=f"old{i}") for i in range(TILES)]
        raws = [keep.tile([P, PACK, HALF], F32, name=f"raw{h}") for h in range(2)]
        xa_sb = keep.tile([P, 2 * J], U8, name="xa_sb", align_bytes=64)
        wa_sb = keep.tile([P, 4 * N], U8, name="wa_sb", align_bytes=64)
        wb_sb = keep.tile([P, 2 * N], U8, name="wb_sb", align_bytes=64)
        xa_plane = keep.tile([P, J], U8, name="xa_plane", align_bytes=64)
        wa_plane = keep.tile([P, N], U8, name="wa_plane", align_bytes=64)
        wb_plane = keep.tile([P, N], U8, name="wb_plane", align_bytes=64)

        def load_plane(queue, plane, scales):
            for q in range(QUADRANTS):
                queue.dma_start(
                    out=plane[32 * q : 32 * q + 4, :].bitcast(I32),
                    in_=scales[0, 4 * q : 4 * q + 4, :].bitcast(I32),
                )

        def load_old(i):
            nc.sync.dma_start(out=olds[i][:], in_=old[i * P : (i + 1) * P, :])

        xb_rows = xb.rearrange("(p r) j -> p r j", r=PACK)
        load_plane(nc.gpsimd, xa_plane, xa_scales)
        nc.sync.dma_start(out=raws[0][:], in_=xb_rows[:, :, 0:HALF])
        nc.sync.dma_start(offsets[:], offs)
        load_plane(nc.sync, wb_plane, wb_scales)
        nc.sync.dma_start(out=raws[1][:], in_=xb_rows[:, :, HALF:J])
        load_old(0)
        nc.sync.dma_start(out=wb_sb[:].bitcast(I32), in_=wb_words[0].bitcast(I32))
        load_plane(nc.sync, wa_plane, wa_scales)
        nc.sync.dma_start(out=xa_sb[:].bitcast(I32), in_=xa_words[0].bitcast(I32))
        nc.sync.dma_start(out=wa_sb[:].bitcast(I32), in_=wa_words[0].rearrange("p n t -> p (n t)").bitcast(I32))
        for i in range(1, TILES):
            load_old(i)

        xb_codes = keep.tile([P, J], U32, name="xb_codes", align_bytes=64)
        xb_plane = keep.tile([P, J], U8, name="xb_plane", align_bytes=64)
        for h in range(2):
            grouped = keep.tile([P, HALF, PACK], BF16, name=f"grouped{h}", align_bytes=64)
            for copy, first, end in ((nc.scalar.copy, WEAVE_SPLIT, HALF), (nc.vector.tensor_copy, 0, WEAVE_SPLIT)):
                copy(
                    out=grouped[:, first:end, :].rearrange("p (c i) r -> p c r i", i=4),
                    in_=raws[h][:, :, first:end].rearrange("p r (c i) -> p c r i", i=4),
                )
            cols = slice(h * HALF, (h + 1) * HALF)
            nc.vector.quantize_mx(
                out=xb_codes[:, cols].bitcast(FP8X4),
                scales=xb_plane[:, cols],
                in_=grouped[:].rearrange("p j r -> p (j r)"),
            )

        fds = [keep.tile([P, T], F32, name=f"fd{i}") for i in range(TILES)]
        nc.vector.tensor_scalar(out=fds[0][:, 0:FADE_SPLIT], in0=olds[0][:, 0:FADE_SPLIT], scalar1=FADE, scalar2=None, op0=ALU.mult)
        nc.scalar.mul(out=fds[0][:, FADE_SPLIT:T], in_=olds[0][:, FADE_SPLIT:T], mul=FADE)
        pages = [keep.tile([P, T], F32, name="page0", tag="old0")]
        nc.gpsimd.memset(pages[0][:], 0.0)
        picked = keep.tile([P, J], F32, name="picked", tag="picked")
        minus_picked = keep.tile([P, J], F32, name="minus_picked", tag="minus_picked")
        for h in range(2):
            cols = slice(h * HALF, (h + 1) * HALF)
            nc.vector.tensor_copy(picked[:, cols], fds[0][:].indirect(offsets[:, h * HALF // GROUP : (h + 1) * HALF // GROUP]))
            nc.scalar.mul(out=minus_picked[:, cols], in_=picked[:, cols], mul=-1.0)

        banks = [psum.tile([P, J], F32, name=f"bank{i}") for i in range(TILES)]

        def pass_a(i, start, stop):
            nc.tensor.matmul_mx(
                out=banks[i][:],
                lhsT=wa_sb[:, 4 * i * P : 4 * (i + 1) * P].bitcast(FP8X4),
                lhsT_scale=wa_plane[:, i * P : (i + 1) * P],
                rhs=xa_sb[:].bitcast(FP4X4),
                rhs_scale=xa_plane[:],
                start=start,
                stop=stop,
            )

        def pass_b(i, start, stop):
            nc.tensor.matmul_mx(
                out=banks[i][:],
                lhsT=wb_sb[:, 2 * i * P : 2 * (i + 1) * P].bitcast(FP4X4),
                lhsT_scale=wb_plane[:, i * P : (i + 1) * P],
                rhs=xb_codes[:].bitcast(FP8X4),
                rhs_scale=xb_plane[:],
                start=start,
                stop=stop,
            )

        pass_b(0, True, False)
        pass_a(0, False, True)
        for i in range(1, TILES):
            pass_a(i, True, False)
            pass_b(i, False, True)

        peak = keep.tile([P, J], F32, name="peak", tag="peak")
        nc.vector.tensor_tensor(out=peak[:], in0=banks[0][:], in1=picked[:], op=ALU.max)
        nc.vector.tensor_tensor(pages[0][:].indirect(offsets[:]), peak[:], minus_picked[:], ALU.add)

        for i, tag in enumerate(("picked", "minus_picked", "peak")):
            page = keep.tile([P, T], F32, name=f"page{i + 1}", tag=tag)
            nc.gpsimd.memset(page[:], 0.0)
            pages.append(page)

        nc.scalar.mul(out=fds[1][:], in_=olds[1][:], mul=FADE)
        sum_one = keep.tile([P, J], F32, name="sum_one", tag="old1")
        nc.scalar.copy(out=sum_one[:], in_=banks[1][:])
        nc.scalar.mul(out=fds[2][:], in_=olds[2][:], mul=FADE)
        sum_pair = keep.tile([P, 2 * J], F32, name="sum_pair", tag="old2")
        sums = {1: sum_one[:], 2: sum_pair[:, 0:J], 3: sum_pair[:, J : 2 * J]}
        nc.scalar.copy(out=sums[2], in_=banks[2][:])
        nc.scalar.copy(out=sums[3], in_=banks[3][:])
        nc.scalar.mul(out=fds[3][:], in_=olds[3][:], mul=FADE)

        gaps = {}
        for i in range(1, TILES):
            gaps[i] = keep.tile([P, J], F32, name=f"gap{i}")
            nc.vector.tensor_tensor(gaps[i][:], fds[i][:].indirect(offsets[:]), sums[i], ALU.subtract)

        def add_and_store(i):
            tag = "old2" if i == 0 else f"new{i}"
            new = keep.tile([P, T], F32, name=f"new{i}", tag=tag)
            nc.gpsimd.tensor_tensor(out=new[:], in0=fds[i][:], in1=pages[i][:], op=ALU.add)
            nc.sync.dma_start(out=out[i * P : (i + 1) * P, :], in_=new[:])

        rises = keep.tile([P, LAST * J], F32, name="rises", tag="old3")
        for i in range(1, TILES):
            rise = rises[:, (i - 1) * J : i * J]
            nc.scalar.activation(out=rise, in_=gaps[i][:], func=ACT.Relu, scale=-1.0)
            add_and_store(i - 1)
            nc.vector.tensor_copy(pages[i][:].indirect(offsets[:]), rise)

        width = T // TAIL_PIECES
        for piece in range(TAIL_PIECES):
            cols = slice(piece * width, (piece + 1) * width)
            tail = keep.tile([P, width], F32, name=f"tail{piece}")
            nc.vector.tensor_tensor(out=tail[:], in0=fds[LAST][:, cols], in1=pages[LAST][:, cols], op=ALU.add)
            nc.scalar.dma_start(out=out[LAST * P : N, cols], in_=tail[:])
